import numpy as np
import ml_dtypes


def mxq(x, axis, fmt="e4m3"):
    dtype, down = {"e4m3": (ml_dtypes.float8_e4m3fn, 7), "e5m2": (ml_dtypes.float8_e5m2, 14)}[fmt]
    v = np.moveaxis(np.asarray(x, np.float32).astype(ml_dtypes.bfloat16).astype(np.float64), axis, -1)
    blocks = v.reshape(v.shape[:-1] + (-1, 32))
    amax = np.abs(blocks).max(-1, keepdims=True)
    byte = np.maximum(np.where(amax > 0, np.frexp(amax)[1] - 1 + 127, 0) - down, 1)
    scale = np.exp2(byte - 127.0)
    codes = (blocks / scale).astype(np.float32).astype(dtype).astype(np.float64)
    return np.moveaxis((codes * scale).reshape(v.shape), -1, axis)


WIDE = False


def mx_kscale(k):
    if not WIDE:
        return np.ones(k)
    levels = np.array([10, -10, 5, -5, 0])
    if k % 512:
        return np.exp2(np.random.permutation(np.resize(levels, k // 32))).repeat(32)
    a = np.empty((k // 512, 16))
    for p in range(k // 512):
        a[p, :8] = np.random.permutation(np.resize(levels, 8))
        for g in range(8):
            far = levels[np.abs(levels - a[p, g]) >= 10]
            a[p, g + 8] = far[np.random.randint(len(far))]
    return np.exp2(a.ravel()).repeat(32)


def f64(x):
    return np.asarray(x).astype(np.float64)


def striped(idx):
    return np.tile(np.asarray(idx).reshape(-1, 16).T, (8, 1)).astype(np.uint16)


def unstriped(offs):
    return offs[:16].T.reshape(-1).astype(np.int64)


E2M1 = np.array([0.0, 0.5, 1.0, 1.5, 2.0, 3.0, 4.0, 6.0, -0.0, -0.5, -1.0, -1.5, -2.0, -3.0, -4.0, -6.0])


def pack_weight(w, fmt):
    k, n = w.shape
    w = f64(np.asarray(w, np.float32).astype(ml_dtypes.bfloat16)).reshape(k // 32, 32, n)
    amax = np.abs(w).max(1)
    if fmt == "e4m3":
        byte = np.frexp(amax)[1] - 1 + 127 - 7
    else:
        mant, ex = np.frexp(amax / 6.0)
        byte = np.where(mant > 0.5, ex, ex - 1) + 127
    byte = np.clip(np.where(amax > 0, byte, 1), 1, 254)
    scaled = (w * np.exp2(127.0 - byte)[:, None, :]).reshape(k, n).astype(np.float32)
    by_word = np.ascontiguousarray(scaled.reshape(k // 512, 128, 4, n).transpose(0, 1, 3, 2))
    if fmt == "e4m3":
        words = by_word.astype(ml_dtypes.float8_e4m3fn).view(np.uint8)
    else:
        c = by_word.astype(ml_dtypes.float4_e2m1fn).view(np.uint8) & 0xF
        words = (c[..., 0::2] | (c[..., 1::2] << 4)).reshape(k // 512, 128, 2 * n)
    return np.ascontiguousarray(words), np.ascontiguousarray(byte.astype(np.uint8).reshape(k // 512, 16, n))


def unpack_weight(words, scales, fmt):
    g, _, n = scales.shape
    words = np.ascontiguousarray(words).reshape(g, 128, n, -1)
    if fmt == "e4m3":
        vals = words.view(ml_dtypes.float8_e4m3fn).astype(np.float64)
    else:
        nib = np.empty((g, 128, n, 4), np.uint8)
        nib[..., 0::2] = words & 0xF
        nib[..., 1::2] = words >> 4
        vals = E2M1[nib]
    vals = vals * np.repeat(np.exp2(scales.astype(np.float64) - 127.0), 8, axis=1)[..., None]
    return vals.transpose(0, 1, 3, 2).reshape(g * 512, n)


D, T, I, Q, E = 512, 1024, 512, 512, 512


def setup_inputs():
    n = np.random.standard_normal
    idx = np.random.permutation(T)[:I]
    fd = mx_kscale(D)
    fq = mx_kscale(Q)
    keysp = pack_weight(n((D, T)) / fd[:, None], "e2m1")
    return {
        "query": (n((D, Q)) * 0.25 / np.sqrt(D) * fd[:, None]).astype(np.float32),
        "keys_words": keysp[0],
        "keys_scales": keysp[1],
        "fac": (np.random.uniform(0.5, 2.0, (Q, 1)) * fq[:, None]).astype(np.float32),
        "erase": (4.0 * np.random.uniform(0.0, 1.0, (Q, E)) ** 8 / fq[:, None]).astype(np.float32),
        "add": (n((Q, E)) / fq[:, None]).astype(np.float32),
        "ef": (np.random.uniform(0.2, 0.8, (E, 1))).astype(np.float32),
        "mem": (n((E, T))).astype(np.float32),
        "retain": (np.random.uniform(0.0, 1.0, (1, T))).astype(np.float32),
        "offs": striped(idx),
    }


def reference(query, keys_words, keys_scales, fac, erase, add, ef, mem, retain, offs):
    idx = unstriped(offs)
    keysu = unpack_weight(keys_words, keys_scales, "e2m1")
    queryq = mxq(f64(query), 0, "e4m3")
    keysidxg = keysu[:, idx]
    a = queryq.T @ keysidxg
    p = np.exp(a - np.max(a, axis=1, keepdims=True))
    w = p * f64(fac) / np.sum(p, axis=1, keepdims=True)
    eraseq = mxq(f64(erase), 0, "e4m3")
    wq = mxq(w, 0, "e4m3")
    er = eraseq.T @ wq
    addq = mxq(f64(add), 0, "e4m3")
    ad = addq.T @ wq
    x = f64(mem)[:, idx] * (1.0 - f64(ef) * er) + ad
    xf = np.zeros((E, T))
    xf[:, idx] = x
    y = f64(mem) * f64(retain) + xf
    return y

@@ -1,0 +1,275 @@
+from contextlib import ExitStack
+
+import concourse.mybir as mybir
+from concourse.masks import make_identity
+
+D, T, I, Q, E = 512, 1024, 512, 512, 512
+FLOPS = 2 * D * Q * I + 2 * 2 * Q * E * I
+
+F32 = mybir.dt.float32
+BF16 = mybir.dt.bfloat16
+I32 = mybir.dt.int32
+U32 = mybir.dt.uint32
+U16 = mybir.dt.uint16
+U8 = mybir.dt.uint8
+FP8X4 = mybir.dt.float8_e4m3fn_x4
+FP4X4 = mybir.dt.float4_e2m1fn_x4
+ALU = mybir.AluOpType
+ACT = mybir.ActivationFunctionType
+AX = mybir.AxisListType
+
+P = 128
+PACK = 4
+E_TILES = E // P
+T_BLOCKS = T // P
+BANK = 512
+HALF_I = I // 2
+HALF_E = E // 2
+
+
+def tile_attend_ntmwrite_kernel(tc, query, keys_words, keys_scales, fac, erase, add, ef, mem, retain, offs, out):
+    nc = tc.nc
+    with ExitStack() as ctx:
+        keep = ctx.enter_context(tc.tile_pool(name="keep", bufs=1))
+        ring = ctx.enter_context(tc.tile_pool(name="ring", bufs=2))
+        psum = ctx.enter_context(tc.psum_pool(name="psum", bufs=1))
+        banks = [psum.tile([P, BANK], F32, name="bank%d" % n) for n in range(8)]
+
+        def held(shape, dtype, name, tag=None):
+            return keep.tile(shape, dtype, name=name, tag=tag or name, align_bytes=64)
+
+        offsets = keep.tile([P, I // 16], U16, name="offsets")
+        nc.sync.dma_start(offsets[:], offs)
+        key_scales = held([P, T], U8, "key_scales")
+        nc.gpsimd.memset(key_scales[:].bitcast(I32), 0)
+        key_words = held([P, T], U16, "key_words")
+        nc.sync.dma_start(key_words[:].bitcast(I32), keys_words[0].bitcast(I32))
+        for quad in range(4):
+            nc.sync.dma_start(
+                key_scales[32 * quad : 32 * quad + 4, :].bitcast(I32),
+                keys_scales[0, 4 * quad : 4 * quad + 4, :].bitcast(I32),
+            )
+        query_raw = held([P, PACK, Q], F32, "query_raw")
+        nc.sync.dma_start(query_raw[:], query.rearrange("(p j) q -> p j q", j=PACK))
+        fac_cols = held([P, PACK], F32, "fac_cols")
+        nc.sync.dma_start(fac_cols[:], fac.rearrange("(p r) o -> p (r o)", r=PACK))
+        vec_rows = held([P, P], F32, "vec_rows")
+        nc.gpsimd.memset(vec_rows[:], 0.0)
+        nc.gpsimd.dma_start(vec_rows[0:T_BLOCKS, :], retain.rearrange("o (b t) -> (o b) t", t=P))
+        nc.gpsimd.dma_start(vec_rows[T_BLOCKS : T_BLOCKS + E_TILES, :], ef.rearrange("(j p) o -> j (p o)", p=P))
+        erase_raw, add_raw, mem_tiles = [], [], []
+        for pair in range(2):
+            cols = slice(pair * HALF_E, (pair + 1) * HALF_E)
+            for name, src, tiles in (("erase_raw", erase, erase_raw), ("add_raw", add, add_raw)):
+                raw = held([P, PACK, HALF_E], F32, "%s%d" % (name, pair))
+                nc.sync.dma_start(raw[:], src.rearrange("(p r) e -> p r e", r=PACK)[:, :, cols])
+                tiles.append(raw)
+            for j in (2 * pair, 2 * pair + 1):
+                mem_j = held([P, T], F32, "mem%d" % j)
+                nc.sync.dma_start(mem_j[:], mem[j * P : (j + 1) * P, :])
+                mem_tiles.append(mem_j)
+
+        zero_col = held([P, 1], F32, "zero_col")
+        nc.vector.memset(zero_col[:], 0.0)
+        one_col = held([P, 1], F32, "one_col")
+        nc.scalar.activation(one_col[:], zero_col[:], ACT.Exp)
+
+        identity = held([P, P], F32, "identity")
+        make_identity(nc, identity[:])
+        placed = []
+        for j in range(2):
+            placed_j = held([P, T], F32, "placed%d" % j)
+            nc.vector.memset(placed_j[:], 0.0)
+            placed.append(placed_j)
+
+        listed_words = held([P, I], U16, "listed_words")
+        nc.vector.tensor_copy(listed_words[:], key_words[:].indirect(offsets[:]))
+        listed_scales = held([P, I], U8, "listed_scales")
+        nc.vector.tensor_copy(listed_scales[:], key_scales[:].indirect(offsets[:]))
+
+        def quantise(grouped, name):
+            width = grouped.shape[1]
+            codes = held([P, width], U32, name + "_codes")
+            scales = held([P, width], U8, name + "_scales")
+            nc.vector.quantize_mx(codes[:].bitcast(FP8X4), scales[:], grouped.rearrange("p c r -> p (c r)"))
+            return codes, scales
+
+        query_by_place = query_raw[:].rearrange("p j (s r) -> p s j r", r=PACK)
+        query_mx = []
+        for pair in range(2):
+            grouped = held([P, 2 * P, PACK], BF16, "query_grouped%d" % pair)
+            src = query_by_place[:, :, :, 2 * pair : 2 * pair + 2]
+            dst = grouped[:].rearrange("p (r s) j -> p s j r", r=2)
+            if pair == 0:
+                nc.vector.tensor_copy(dst, src)
+            else:
+                nc.scalar.copy(dst, src)
+            query_mx.append(quantise(grouped[:], "query%d" % pair))
+
+        def group_heads(engine_copy, raw, name, tag=None):
+            grouped = held([P, HALF_E, PACK], BF16, name, tag)
+            for jj in range(2):
+                cols = slice(jj * P, (jj + 1) * P)
+                engine_copy(
+                    grouped[:, cols, :].rearrange("p (c i) r -> p c r i", i=2),
+                    raw[:, :, cols].rearrange("p r (c i) -> p c r i", i=2),
+                )
+            return grouped
+
+        neg_max = held([P, PACK], F32, "neg_max")
+        sums = held([P, PACK], F32, "sums")
+        probs = held([P, PACK, I], F32, "probs")
+        for r in range(PACK):
+            scores = banks[r]
+            codes, scales = query_mx[r // 2]
+            cols = slice((r % 2) * P, (r % 2 + 1) * P)
+            nc.tensor.matmul_mx(
+                out=scores[:],
+                lhsT=codes[:, cols].bitcast(FP8X4),
+                lhsT_scale=scales[:, cols],
+                rhs=listed_words[:].bitcast(FP4X4),
+                rhs_scale=listed_scales[:],
+                start=True,
+                stop=True,
+            )
+            nc.vector.tensor_reduce(neg_max[:, r : r + 1], scores[:], AX.X, ALU.max, negate=True)
+            nc.scalar.activation(
+                probs[:, r, :], scores[:], ACT.Exp, bias=neg_max[:, r : r + 1], accum_out=sums[:, r : r + 1]
+            )
+        for j, tag in ((2, "query_grouped1"), (3, "query0_codes")):
+            placed_j = held([P, T], F32, "placed%d" % j, tag)
+            nc.gpsimd.memset(placed_j[:], 0.0)
+            placed.append(placed_j)
+        erase_grouped0 = group_heads(nc.scalar.copy, erase_raw[0], "erase_grouped0")
+        add_grouped0 = group_heads(nc.vector.tensor_copy, add_raw[0], "add_grouped0", "query1_codes")
+        inv_sums = held([P, PACK], F32, "inv_sums")
+        nc.vector.reciprocal(inv_sums[:], sums[:])
+        gains = held([P, PACK], F32, "gains")
+        nc.vector.tensor_tensor(gains[:], inv_sums[:], fac_cols[:], ALU.mult)
+        heads_mx = [(quantise(erase_grouped0[:], "erase0"), quantise(add_grouped0[:], "add0"))]
+
+        w_codes = held([P, I], U32, "w_codes")
+        w_scales = held([P, I], U8, "w_scales")
+        gains_spread = gains[:].unsqueeze(1).unsqueeze(3).to_broadcast([P, HALF_I // 2, PACK, 2])
+        w_rows = held([P, PACK, HALF_I], BF16, "w_rows")
+        for r in range(PACK):
+            nc.scalar.activation(w_rows[:, r, :], probs[:, r, HALF_I:I], ACT.Copy, scale=gains[:, r : r + 1])
+        for half in range(2):
+            cols = slice(half * HALF_I, (half + 1) * HALF_I)
+            w_grouped = held([P, HALF_I, PACK], BF16, "w_grouped%d" % half)
+            if half == 0:
+                nc.vector.tensor_tensor(
+                    w_grouped[:].rearrange("p (c i) r -> p c r i", i=2),
+                    probs[:, :, cols].rearrange("p r (c i) -> p c r i", i=2),
+                    gains_spread,
+                    ALU.mult,
+                )
+            else:
+                nc.vector.tensor_copy(
+                    w_grouped[:].rearrange("p (c i) r -> p c r i", i=4),
+                    w_rows[:].rearrange("p r (c i) -> p c r i", i=4),
+                )
+            nc.vector.quantize_mx(
+                w_codes[:, cols].bitcast(FP8X4), w_scales[:, cols], w_grouped[:].rearrange("p i r -> p (i r)")
+            )
+
+        nc.tensor.transpose(banks[3][:, 0:P], vec_rows[:], identity[:])
+        retain_cols = held([P, T_BLOCKS], F32, "retain_cols")
+        nc.scalar.copy(retain_cols[:], banks[3][:, 0:T_BLOCKS])
+        neg_ef_cols = held([P, E_TILES], F32, "neg_ef_cols")
+        nc.scalar.activation(neg_ef_cols[:], banks[3][:, T_BLOCKS : T_BLOCKS + E_TILES], ACT.Copy, scale=-1.0)
+
+        def retain_turned(pair, turn_banks):
+            turned = held([P, T_BLOCKS, HALF_E], F32, "retained_t%d" % pair)
+            for b in range(T_BLOCKS):
+                bank = turn_banks[(b // 2) % len(turn_banks)]
+                lo = (b % 2) * HALF_E
+                for jj in range(2):
+                    nc.tensor.transpose(
+                        bank[:, lo + jj * P : lo + (jj + 1) * P],
+                        mem_tiles[2 * pair + jj][:, b * P : (b + 1) * P],
+                        identity[:],
+                    )
+                if b % 2 == 1:
+                    for bb in (b - 1, b):
+                        lo = (bb % 2) * HALF_E
+                        nc.scalar.activation(
+                            turned[:, bb, :], bank[:, lo : lo + HALF_E], ACT.Copy, scale=retain_cols[:, bb : bb + 1]
+                        )
+            return turned
+
+        def write_listed(j, cols, sum_banks):
+            width = cols.stop - cols.start
+            e_cols = slice((j % 2) * P, (j % 2 + 1) * P)
+            for (codes, scales), bank in zip(heads_mx[j // 2], sum_banks):
+                nc.tensor.matmul_mx(
+                    out=bank[:, 0:width],
+                    lhsT=codes[:, e_cols].bitcast(FP8X4),
+                    lhsT_scale=scales[:, e_cols],
+                    rhs=w_codes[:, cols].bitcast(FP8X4),
+                    rhs_scale=w_scales[:, cols],
+                    start=True,
+                    stop=True,
+                )
+            kept = held([P, width], F32, "kept%d_%d" % (j, cols.start))
+            nc.scalar.activation(
+                kept[:], sum_banks[0][:, 0:width], ACT.Identity, bias=one_col[:], scale=neg_ef_cols[:, j : j + 1]
+            )
+            added = held([P, width], F32, "added%d_%d" % (j, cols.start))
+            nc.scalar.copy(added[:], sum_banks[1][:, 0:width])
+            listed = offsets[:, cols.start // 16 : cols.stop // 16]
+            left = ring.tile([P, width], F32, name="left")
+            nc.vector.tensor_tensor(left[:], mem_tiles[j][:].indirect(listed), kept[:], ALU.mult)
+            nc.vector.tensor_tensor(placed[j][:].indirect(listed), left[:], added[:], ALU.add)
+
+        def finish(j, retained_t):
+            last = j == E_TILES - 1
+            e_cols = slice((j % 2) * P, (j % 2 + 1) * P)
+            for half in range(2):
+                blocks = range(4 * half, 4 * half + 4)
+                cols = slice(half * BANK, (half + 1) * BANK)
+                back = banks[(4 if last else 2) + half]
+                for n, b in enumerate(blocks):
+                    nc.tensor.matmul(
+                        back[:, n * P : (n + 1) * P],
+                        retained_t[:, b, e_cols],
+                        identity[:],
+                        start=n == 0,
+                        stop=last and n == 3,
+                        is_transpose=True,
+                    )
+                result = ring.tile([P, BANK], F32, name="result", bufs=4)
+                if last:
+                    nc.vector.tensor_tensor(result[:], back[:], placed[j][:, cols], ALU.add)
+                else:
+                    bank = banks[half]
+                    for n, b in enumerate(blocks):
+                        nc.tensor.transpose(bank[:, n * P : (n + 1) * P], placed[j][:, b * P : (b + 1) * P], identity[:])
+                    placed_t = ring.tile([P, BANK], F32, name="placed_t")
+                    nc.scalar.copy(placed_t[:], bank[:])
+                    for n in range(4):
+                        nc.tensor.matmul(
+                            back[:, n * P : (n + 1) * P],
+                            placed_t[:, n * P : (n + 1) * P],
+                            identity[:],
+                            start=False,
+                            stop=n == 3,
+                            is_transpose=True,
+                        )
+                    nc.scalar.copy(result[:], back[:])
+                nc.sync.dma_start(out[j * P : (j + 1) * P, cols], result[:])
+
+        retained_low = retain_turned(0, banks[0:3])
+        write_listed(0, slice(0, HALF_I), banks[4:6])
+        write_listed(0, slice(HALF_I, I), banks[6:8])
+        write_listed(1, slice(0, I), banks[4:6])
+        erase_grouped1 = group_heads(nc.scalar.copy, erase_raw[1], "erase_grouped1", "w_grouped0")
+        add_grouped1 = group_heads(nc.scalar.copy, add_raw[1], "add_grouped1", "w_grouped1")
+        heads_mx.append((quantise(erase_grouped1[:], "erase1"), quantise(add_grouped1[:], "add1")))
+        write_listed(2, slice(0, I), banks[6:8])
+        write_listed(3, slice(0, I), banks[4:6])
+        finish(0, retained_low)
+        retained_high = retain_turned(1, banks[6:8])
+        finish(1, retained_low)
+        finish(2, retained_high)
+        finish(3, retained_high)

@@ -64,10 +64,10 @@ def tile_attend_ntmwrite_kernel(tc, query, keys_words, keys_scales, fac, erase, 
                 raw = held([P, PACK, HALF_E], F32, "%s%d" % (name, pair))
                 nc.sync.dma_start(raw[:], src.rearrange("(p r) e -> p r e", r=PACK)[:, :, cols])
                 tiles.append(raw)
-            for j in (2 * pair, 2 * pair + 1):
-                mem_j = held([P, T], F32, "mem%d" % j)
-                nc.sync.dma_start(mem_j[:], mem[j * P : (j + 1) * P, :])
-                mem_tiles.append(mem_j)
+        for j in range(E_TILES):
+            mem_j = held([P, T], F32, "mem%d" % j)
+            nc.sync.dma_start(mem_j[:], mem[j * P : (j + 1) * P, :])
+            mem_tiles.append(mem_j)
 
         zero_col = held([P, 1], F32, "zero_col")
         nc.vector.memset(zero_col[:], 0.0)
@@ -179,26 +179,16 @@ def tile_attend_ntmwrite_kernel(tc, query, keys_words, keys_scales, fac, erase, 
         neg_ef_cols = held([P, E_TILES], F32, "neg_ef_cols")
         nc.scalar.activation(neg_ef_cols[:], banks[3][:, T_BLOCKS : T_BLOCKS + E_TILES], ACT.Copy, scale=-1.0)
 
-        def retain_turned(pair, turn_banks):
-            turned = held([P, T_BLOCKS, HALF_E], F32, "retained_t%d" % pair)
+        def retain_turned(turn_banks):
+            turned = held([P, T_BLOCKS, E], F32, "retained_t")
             for b in range(T_BLOCKS):
-                bank = turn_banks[(b // 2) % len(turn_banks)]
-                lo = (b % 2) * HALF_E
-                for jj in range(2):
-                    nc.tensor.transpose(
-                        bank[:, lo + jj * P : lo + (jj + 1) * P],
-                        mem_tiles[2 * pair + jj][:, b * P : (b + 1) * P],
-                        identity[:],
-                    )
-                if b % 2 == 1:
-                    for bb in (b - 1, b):
-                        lo = (bb % 2) * HALF_E
-                        nc.scalar.activation(
-                            turned[:, bb, :], bank[:, lo : lo + HALF_E], ACT.Copy, scale=retain_cols[:, bb : bb + 1]
-                        )
+                bank = turn_banks[b % 2]
+                for j in range(E_TILES):
+                    nc.tensor.transpose(bank[:, j * P : (j + 1) * P], mem_tiles[j][:, b * P : (b + 1) * P], identity[:])
+                nc.scalar.activation(turned[:, b, :], bank[:], ACT.Copy, scale=retain_cols[:, b : b + 1])
             return turned
 
-        def write_listed(j, cols, sum_banks):
+        def write_listed(j, cols, sum_banks, left_tag):
             width = cols.stop - cols.start
             e_cols = slice((j % 2) * P, (j % 2 + 1) * P)
             for (codes, scales), bank in zip(heads_mx[j // 2], sum_banks):
@@ -218,17 +208,17 @@ def tile_attend_ntmwrite_kernel(tc, query, keys_words, keys_scales, fac, erase, 
             added = held([P, width], F32, "added%d_%d" % (j, cols.start))
             nc.scalar.copy(added[:], sum_banks[1][:, 0:width])
             listed = offsets[:, cols.start // 16 : cols.stop // 16]
-            left = ring.tile([P, width], F32, name="left")
+            left = held([P, width], F32, "left%d_%d" % (j, cols.start), left_tag)
             nc.vector.tensor_tensor(left[:], mem_tiles[j][:].indirect(listed), kept[:], ALU.mult)
             nc.vector.tensor_tensor(placed[j][:].indirect(listed), left[:], added[:], ALU.add)
 
         def finish(j, retained_t):
             last = j == E_TILES - 1
-            e_cols = slice((j % 2) * P, (j % 2 + 1) * P)
+            e_cols = slice(j * P, (j + 1) * P)
             for half in range(2):
                 blocks = range(4 * half, 4 * half + 4)
                 cols = slice(half * BANK, (half + 1) * BANK)
-                back = banks[(4 if last else 2) + half]
+                back = banks[2 * (j % 2) + half]
                 for n, b in enumerate(blocks):
                     nc.tensor.matmul(
                         back[:, n * P : (n + 1) * P],
@@ -242,7 +232,7 @@ def tile_attend_ntmwrite_kernel(tc, query, keys_words, keys_scales, fac, erase, 
                 if last:
                     nc.vector.tensor_tensor(result[:], back[:], placed[j][:, cols], ALU.add)
                 else:
-                    bank = banks[half]
+                    bank = banks[4 + half]
                     for n, b in enumerate(blocks):
                         nc.tensor.transpose(bank[:, n * P : (n + 1) * P], placed[j][:, b * P : (b + 1) * P], identity[:])
                     placed_t = ring.tile([P, BANK], F32, name="placed_t")
@@ -259,17 +249,14 @@ def tile_attend_ntmwrite_kernel(tc, query, keys_words, keys_scales, fac, erase, 
                     nc.scalar.copy(result[:], back[:])
                 nc.sync.dma_start(out[j * P : (j + 1) * P, cols], result[:])
 
-        retained_low = retain_turned(0, banks[0:3])
-        write_listed(0, slice(0, HALF_I), banks[4:6])
-        write_listed(0, slice(HALF_I, I), banks[6:8])
-        write_listed(1, slice(0, I), banks[4:6])
-        erase_grouped1 = group_heads(nc.scalar.copy, erase_raw[1], "erase_grouped1", "w_grouped0")
-        add_grouped1 = group_heads(nc.scalar.copy, add_raw[1], "add_grouped1", "w_grouped1")
+        write_listed(0, slice(0, HALF_I), banks[4:6], None)
+        write_listed(0, slice(HALF_I, I), banks[6:8], None)
+        erase_grouped1 = group_heads(nc.scalar.copy, erase_raw[1], "erase_grouped1", "neg_max")
+        add_grouped1 = group_heads(nc.scalar.copy, add_raw[1], "add_grouped1", "w_rows")
         heads_mx.append((quantise(erase_grouped1[:], "erase1"), quantise(add_grouped1[:], "add1")))
-        write_listed(2, slice(0, I), banks[6:8])
-        write_listed(3, slice(0, I), banks[4:6])
-        finish(0, retained_low)
-        retained_high = retain_turned(1, banks[6:8])
-        finish(1, retained_low)
-        finish(2, retained_high)
-        finish(3, retained_high)
+        write_listed(1, slice(0, I), banks[0:2], "w_rows")
+        write_listed(2, slice(0, I), banks[2:4], None)
+        write_listed(3, slice(0, I), banks[4:6], None)
+        retained_t = retain_turned(banks[6:8])
+        for j in range(E_TILES):
+            finish(j, retained_t)

@@ -55,15 +55,13 @@ def tile_attend_ntmwrite_kernel(tc, query, keys_words, keys_scales, fac, erase, 
         nc.sync.dma_start(fac_cols[:], fac.rearrange("(p r) o -> p (r o)", r=PACK))
         vec_rows = held([P, P], F32, "vec_rows")
         nc.gpsimd.memset(vec_rows[:], 0.0)
-        nc.gpsimd.dma_start(vec_rows[0:T_BLOCKS, :], retain.rearrange("o (b t) -> (o b) t", t=P))
-        nc.gpsimd.dma_start(vec_rows[T_BLOCKS : T_BLOCKS + E_TILES, :], ef.rearrange("(j p) o -> j (p o)", p=P))
-        erase_raw, add_raw, mem_tiles = [], [], []
-        for pair in range(2):
-            cols = slice(pair * HALF_E, (pair + 1) * HALF_E)
-            for name, src, tiles in (("erase_raw", erase, erase_raw), ("add_raw", add, add_raw)):
-                raw = held([P, PACK, HALF_E], F32, "%s%d" % (name, pair))
-                nc.sync.dma_start(raw[:], src.rearrange("(p r) e -> p r e", r=PACK)[:, :, cols])
-                tiles.append(raw)
+        nc.sync.dma_start(vec_rows[0:T_BLOCKS, :], retain.rearrange("o (b t) -> (o b) t", t=P))
+        nc.sync.dma_start(vec_rows[T_BLOCKS : T_BLOCKS + E_TILES, :], ef.rearrange("(j p) o -> j (p o)", p=P))
+        erase_raw = held([P, PACK, E], F32, "erase_raw")
+        nc.sync.dma_start(erase_raw[:], erase.rearrange("(p r) e -> p r e", r=PACK))
+        add_raw = held([P, PACK, E], F32, "add_raw")
+        nc.sync.dma_start(add_raw[:], add.rearrange("(p r) e -> p r e", r=PACK))
+        mem_tiles = []
         for j in range(E_TILES):
             mem_j = held([P, T], F32, "mem%d" % j)
             nc.sync.dma_start(mem_j[:], mem[j * P : (j + 1) * P, :])
@@ -77,9 +75,9 @@ def tile_attend_ntmwrite_kernel(tc, query, keys_words, keys_scales, fac, erase, 
         identity = held([P, P], F32, "identity")
         make_identity(nc, identity[:])
         placed = []
-        for j in range(2):
+        for j in range(3):
             placed_j = held([P, T], F32, "placed%d" % j)
-            nc.vector.memset(placed_j[:], 0.0)
+            nc.vector.memset(placed_j[:].bitcast(I32), 0)
             placed.append(placed_j)
 
         listed_words = held([P, I], U16, "listed_words")
@@ -106,18 +104,23 @@ def tile_attend_ntmwrite_kernel(tc, query, keys_words, keys_scales, fac, erase, 
                 nc.scalar.copy(dst, src)
             query_mx.append(quantise(grouped[:], "query%d" % pair))
 
+        placed_last = held([P, T], F32, "placed3", "query_grouped1")
+        nc.gpsimd.memset(placed_last[:], 0.0)
+        placed.append(placed_last)
+
         def group_heads(engine_copy, raw, name, tag=None):
             grouped = held([P, HALF_E, PACK], BF16, name, tag)
             for jj in range(2):
                 cols = slice(jj * P, (jj + 1) * P)
                 engine_copy(
-                    grouped[:, cols, :].rearrange("p (c i) r -> p c r i", i=2),
-                    raw[:, :, cols].rearrange("p r (c i) -> p c r i", i=2),
+                    grouped[:, cols, :].rearrange("p (c i) r -> p c r i", i=4),
+                    raw[:, :, cols].rearrange("p r (c i) -> p c r i", i=4),
                 )
             return grouped
 
         neg_max = held([P, PACK], F32, "neg_max")
-        sums = held([P, PACK], F32, "sums")
+        erase_grouped0 = group_heads(nc.scalar.copy, erase_raw[:, :, 0:HALF_E], "erase_grouped0")
+        sums = erase_raw[:, 0, P : P + PACK]
         probs = held([P, PACK, I], F32, "probs")
         for r in range(PACK):
             scores = banks[r]
@@ -136,21 +139,16 @@ def tile_attend_ntmwrite_kernel(tc, query, keys_words, keys_scales, fac, erase, 
             nc.scalar.activation(
                 probs[:, r, :], scores[:], ACT.Exp, bias=neg_max[:, r : r + 1], accum_out=sums[:, r : r + 1]
             )
-        for j, tag in ((2, "query_grouped1"), (3, "query0_codes")):
-            placed_j = held([P, T], F32, "placed%d" % j, tag)
-            nc.gpsimd.memset(placed_j[:], 0.0)
-            placed.append(placed_j)
-        erase_grouped0 = group_heads(nc.scalar.copy, erase_raw[0], "erase_grouped0")
-        add_grouped0 = group_heads(nc.vector.tensor_copy, add_raw[0], "add_grouped0", "query1_codes")
-        inv_sums = held([P, PACK], F32, "inv_sums")
-        nc.vector.reciprocal(inv_sums[:], sums[:])
-        gains = held([P, PACK], F32, "gains")
-        nc.vector.tensor_tensor(gains[:], inv_sums[:], fac_cols[:], ALU.mult)
+        add_grouped0 = group_heads(nc.vector.tensor_copy, add_raw[:, :, 0:HALF_E], "add_grouped0", "query1_codes")
         heads_mx = [(quantise(erase_grouped0[:], "erase0"), quantise(add_grouped0[:], "add0"))]
+        inv_sums = add_raw[:, 0, P : P + PACK]
+        nc.vector.reciprocal(inv_sums, sums)
+        gains = held([P, PACK], F32, "gains")
+        nc.vector.tensor_tensor(gains[:], inv_sums, fac_cols[:], ALU.mult)
 
         w_codes = held([P, I], U32, "w_codes")
         w_scales = held([P, I], U8, "w_scales")
-        gains_spread = gains[:].unsqueeze(1).unsqueeze(3).to_broadcast([P, HALF_I // 2, PACK, 2])
+        gains_spread = gains[:].unsqueeze(1).unsqueeze(3).to_broadcast([P, HALF_I // 4, PACK, 4])
         w_rows = held([P, PACK, HALF_I], BF16, "w_rows")
         for r in range(PACK):
             nc.scalar.activation(w_rows[:, r, :], probs[:, r, HALF_I:I], ACT.Copy, scale=gains[:, r : r + 1])
@@ -159,8 +157,8 @@ def tile_attend_ntmwrite_kernel(tc, query, keys_words, keys_scales, fac, erase, 
             w_grouped = held([P, HALF_I, PACK], BF16, "w_grouped%d" % half)
             if half == 0:
                 nc.vector.tensor_tensor(
-                    w_grouped[:].rearrange("p (c i) r -> p c r i", i=2),
-                    probs[:, :, cols].rearrange("p r (c i) -> p c r i", i=2),
+                    w_grouped[:].rearrange("p (c i) r -> p c r i", i=4),
+                    probs[:, :, cols].rearrange("p r (c i) -> p c r i", i=4),
                     gains_spread,
                     ALU.mult,
                 )
@@ -182,81 +180,102 @@ def tile_attend_ntmwrite_kernel(tc, query, keys_words, keys_scales, fac, erase, 
         def retain_turned(turn_banks):
             turned = held([P, T_BLOCKS, E], F32, "retained_t")
             for b in range(T_BLOCKS):
-                bank = turn_banks[b % 2]
+                bank = turn_banks[b % len(turn_banks)]
                 for j in range(E_TILES):
                     nc.tensor.transpose(bank[:, j * P : (j + 1) * P], mem_tiles[j][:, b * P : (b + 1) * P], identity[:])
                 nc.scalar.activation(turned[:, b, :], bank[:], ACT.Copy, scale=retain_cols[:, b : b + 1])
             return turned
 
-        def write_listed(j, cols, sum_banks, left_tag):
-            width = cols.stop - cols.start
+        def head_sum(which, j, cols, bank):
+            codes, scales = heads_mx[j // 2][which]
             e_cols = slice((j % 2) * P, (j % 2 + 1) * P)
-            for (codes, scales), bank in zip(heads_mx[j // 2], sum_banks):
-                nc.tensor.matmul_mx(
-                    out=bank[:, 0:width],
-                    lhsT=codes[:, e_cols].bitcast(FP8X4),
-                    lhsT_scale=scales[:, e_cols],
-                    rhs=w_codes[:, cols].bitcast(FP8X4),
-                    rhs_scale=w_scales[:, cols],
-                    start=True,
-                    stop=True,
-                )
+            total = bank[:, 0 : cols.stop - cols.start]
+            nc.tensor.matmul_mx(
+                out=total,
+                lhsT=codes[:, e_cols].bitcast(FP8X4),
+                lhsT_scale=scales[:, e_cols],
+                rhs=w_codes[:, cols].bitcast(FP8X4),
+                rhs_scale=w_scales[:, cols],
+                start=True,
+                stop=True,
+            )
+            return total
+
+        def listed(cols):
+            return offsets[:, cols.start // 16 : cols.stop // 16]
+
+        def erase_listed(j, cols, bank, left_tag=None):
+            width = cols.stop - cols.start
             kept = held([P, width], F32, "kept%d_%d" % (j, cols.start))
             nc.scalar.activation(
-                kept[:], sum_banks[0][:, 0:width], ACT.Identity, bias=one_col[:], scale=neg_ef_cols[:, j : j + 1]
+                kept[:], head_sum(0, j, cols, bank), ACT.Identity, bias=one_col[:], scale=neg_ef_cols[:, j : j + 1]
             )
-            added = held([P, width], F32, "added%d_%d" % (j, cols.start))
-            nc.scalar.copy(added[:], sum_banks[1][:, 0:width])
-            listed = offsets[:, cols.start // 16 : cols.stop // 16]
             left = held([P, width], F32, "left%d_%d" % (j, cols.start), left_tag)
-            nc.vector.tensor_tensor(left[:], mem_tiles[j][:].indirect(listed), kept[:], ALU.mult)
-            nc.vector.tensor_tensor(placed[j][:].indirect(listed), left[:], added[:], ALU.add)
+            nc.vector.tensor_tensor(left[:], mem_tiles[j][:].indirect(listed(cols)), kept[:], ALU.mult)
+            return left
 
-        def finish(j, retained_t):
-            last = j == E_TILES - 1
-            e_cols = slice(j * P, (j + 1) * P)
-            for half in range(2):
-                blocks = range(4 * half, 4 * half + 4)
-                cols = slice(half * BANK, (half + 1) * BANK)
-                back = banks[2 * (j % 2) + half]
-                for n, b in enumerate(blocks):
-                    nc.tensor.matmul(
-                        back[:, n * P : (n + 1) * P],
-                        retained_t[:, b, e_cols],
-                        identity[:],
-                        start=n == 0,
-                        stop=last and n == 3,
-                        is_transpose=True,
-                    )
-                result = ring.tile([P, BANK], F32, name="result", bufs=4)
-                if last:
-                    nc.vector.tensor_tensor(result[:], back[:], placed[j][:, cols], ALU.add)
-                else:
-                    bank = banks[4 + half]
-                    for n, b in enumerate(blocks):
-                        nc.tensor.transpose(bank[:, n * P : (n + 1) * P], placed[j][:, b * P : (b + 1) * P], identity[:])
-                    placed_t = ring.tile([P, BANK], F32, name="placed_t")
-                    nc.scalar.copy(placed_t[:], bank[:])
-                    for n in range(4):
-                        nc.tensor.matmul(
-                            back[:, n * P : (n + 1) * P],
-                            placed_t[:, n * P : (n + 1) * P],
-                            identity[:],
-                            start=False,
-                            stop=n == 3,
-                            is_transpose=True,
-                        )
-                    nc.scalar.copy(result[:], back[:])
-                nc.sync.dma_start(out[j * P : (j + 1) * P, cols], result[:])
+        def add_and_place(j, cols, bank, left):
+            added = held([P, cols.stop - cols.start], F32, "added%d_%d" % (j, cols.start))
+            nc.scalar.copy(added[:], head_sum(1, j, cols, bank))
+            nc.vector.tensor_tensor(placed[j][:].indirect(listed(cols)), left[:], added[:], ALU.add)
 
-        write_listed(0, slice(0, HALF_I), banks[4:6], None)
-        write_listed(0, slice(HALF_I, I), banks[6:8], None)
-        erase_grouped1 = group_heads(nc.scalar.copy, erase_raw[1], "erase_grouped1", "neg_max")
-        add_grouped1 = group_heads(nc.scalar.copy, add_raw[1], "add_grouped1", "w_rows")
+        def turn_back(rows_t, bank, start, stop):
+            for n in range(4):
+                nc.tensor.matmul(
+                    bank[:, n * P : (n + 1) * P],
+                    rows_t[n],
+                    identity[:],
+                    start=start and n == 0,
+                    stop=stop and n == 3,
+                    is_transpose=True,
+                )
+
+        def retained_blocks(j, half):
+            return [retained_t[:, 4 * half + n, j * P : (j + 1) * P] for n in range(4)]
+
+        def store(queue, j, half, result):
+            queue.dma_start(out[j * P : (j + 1) * P, half * BANK : (half + 1) * BANK], result[:])
+
+        def finish_on_vector(j, half, back_bank):
+            result = held([P, BANK], F32, "result%d_%d" % (j, half))
+            nc.vector.tensor_tensor(result[:], back_bank[:], placed[j][:, half * BANK : (half + 1) * BANK], ALU.add)
+            store(nc.sync, j, half, result)
+
+        def finish_on_tensor(j, halves, back_banks, turn_banks):
+            placed_t = []
+            for half, back_bank, turn_bank in zip(halves, back_banks, turn_banks):
+                turn_back(retained_blocks(j, half), back_bank, True, False)
+                for n in range(4):
+                    b = 4 * half + n
+                    nc.tensor.transpose(turn_bank[:, n * P : (n + 1) * P], placed[j][:, b * P : (b + 1) * P], identity[:])
+                turned = held([P, BANK], F32, "placed_t%d_%d" % (j, half))
+                nc.scalar.copy(turned[:], turn_bank[:])
+                placed_t.append(turned)
+            for half, back_bank, turned in zip(halves, back_banks, placed_t):
+                turn_back([turned[:, n * P : (n + 1) * P] for n in range(4)], back_bank, False, True)
+                result = held([P, BANK], F32, "result%d_%d" % (j, half))
+                nc.scalar.copy(result[:], back_bank[:])
+                store(nc.scalar, j, half, result)
+
+        first, second, whole = slice(0, HALF_I), slice(HALF_I, I), slice(0, I)
+        add_and_place(0, first, banks[5], erase_listed(0, first, banks[4]))
+        erase_grouped1 = group_heads(nc.scalar.copy, erase_raw[:, :, HALF_E:E], "erase_grouped1", "neg_max")
+        add_grouped1 = group_heads(nc.scalar.copy, add_raw[:, :, HALF_E:E], "add_grouped1", "fac_cols")
         heads_mx.append((quantise(erase_grouped1[:], "erase1"), quantise(add_grouped1[:], "add1")))
-        write_listed(1, slice(0, I), banks[0:2], "w_rows")
-        write_listed(2, slice(0, I), banks[2:4], None)
-        write_listed(3, slice(0, I), banks[4:6], None)
-        retained_t = retain_turned(banks[6:8])
-        for j in range(E_TILES):
-            finish(j, retained_t)
+        left0 = erase_listed(0, second, banks[6], "fac_cols")
+        left1 = erase_listed(1, whole, banks[2])
+        add_and_place(0, second, banks[7], left0)
+        left2 = erase_listed(2, whole, banks[4])
+        add_and_place(1, whole, banks[3], left1)
+        retained_t = retain_turned(banks[0:2])
+        left3 = erase_listed(3, whole, banks[6])
+        add_and_place(2, whole, banks[5], left2)
+        add_and_place(3, whole, banks[7], left3)
+        on_vector = [(2, 1, banks[5]), (3, 0, banks[6]), (3, 1, banks[7])]
+        finish_on_tensor(0, (0, 1), banks[2:4], banks[0:2])
+        finish_on_tensor(1, (0, 1), banks[2:4], banks[0:2])
+        for j, half, bank in on_vector:
+            turn_back(retained_blocks(j, half), bank, True, True)
+        finish_on_tensor(2, (0,), banks[4:5], banks[3:4])
+        for j, half, bank in on_vector:
+            finish_on_vector(j, half, bank)

from contextlib import ExitStack

import concourse.mybir as mybir
from concourse.masks import make_identity

D, T, I, Q, E = 512, 1024, 512, 512, 512
FLOPS = 2 * D * Q * I + 2 * 2 * Q * E * I

F32 = mybir.dt.float32
BF16 = mybir.dt.bfloat16
I32 = mybir.dt.int32
U32 = mybir.dt.uint32
U16 = mybir.dt.uint16
U8 = mybir.dt.uint8
FP8X4 = mybir.dt.float8_e4m3fn_x4
FP4X4 = mybir.dt.float4_e2m1fn_x4
ALU = mybir.AluOpType
ACT = mybir.ActivationFunctionType
AX = mybir.AxisListType

P = 128
PACK = 4
E_TILES = E // P
T_BLOCKS = T // P
BANK = 512
HALF_I = I // 2
HALF_E = E // 2


def tile_attend_ntmwrite_kernel(tc, query, keys_words, keys_scales, fac, erase, add, ef, mem, retain, offs, out):
    nc = tc.nc
    with ExitStack() as ctx:
        keep = ctx.enter_context(tc.tile_pool(name="keep", bufs=1))
        ring = ctx.enter_context(tc.tile_pool(name="ring", bufs=2))
        psum = ctx.enter_context(tc.psum_pool(name="psum", bufs=1))
        banks = [psum.tile([P, BANK], F32, name="bank%d" % n) for n in range(8)]

        def held(shape, dtype, name, tag=None):
            return keep.tile(shape, dtype, name=name, tag=tag or name, align_bytes=64)

        offsets = keep.tile([P, I // 16], U16, name="offsets")
        nc.sync.dma_start(offsets[:], offs)
        key_scales = held([P, T], U8, "key_scales")
        nc.gpsimd.memset(key_scales[:].bitcast(I32), 0)
        key_words = held([P, T], U16, "key_words")
        nc.sync.dma_start(key_words[:].bitcast(I32), keys_words[0].bitcast(I32))
        for quad in range(4):
            nc.sync.dma_start(
                key_scales[32 * quad : 32 * quad + 4, :].bitcast(I32),
                keys_scales[0, 4 * quad : 4 * quad + 4, :].bitcast(I32),
            )
        query_raw = held([P, PACK, Q], F32, "query_raw")
        nc.sync.dma_start(query_raw[:], query.rearrange("(p j) q -> p j q", j=PACK))
        fac_cols = held([P, PACK], F32, "fac_cols")
        nc.sync.dma_start(fac_cols[:], fac.rearrange("(p r) o -> p (r o)", r=PACK))
        vec_rows = held([P, P], F32, "vec_rows")
        nc.gpsimd.memset(vec_rows[:], 0.0)
        nc.sync.dma_start(vec_rows[0:T_BLOCKS, :], retain.rearrange("o (b t) -> (o b) t", t=P))
        nc.sync.dma_start(vec_rows[T_BLOCKS : T_BLOCKS + E_TILES, :], ef.rearrange("(j p) o -> j (p o)", p=P))
        erase_raw = held([P, PACK, E], F32, "erase_raw")
        nc.sync.dma_start(erase_raw[:], erase.rearrange("(p r) e -> p r e", r=PACK))
        add_raw = held([P, PACK, E], F32, "add_raw")
        nc.sync.dma_start(add_raw[:], add.rearrange("(p r) e -> p r e", r=PACK))
        mem_tiles = []
        for j in range(E_TILES):
            mem_j = held([P, T], F32, "mem%d" % j)
            nc.sync.dma_start(mem_j[:], mem[j * P : (j + 1) * P, :])
            mem_tiles.append(mem_j)

        zero_col = held([P, 1], F32, "zero_col")
        nc.vector.memset(zero_col[:], 0.0)
        one_col = held([P, 1], F32, "one_col")
        nc.scalar.activation(one_col[:], zero_col[:], ACT.Exp)

        identity = held([P, P], F32, "identity")
        make_identity(nc, identity[:])
        placed = []
        for j in range(3):
            placed_j = held([P, T], F32, "placed%d" % j)
            nc.vector.memset(placed_j[:].bitcast(I32), 0)
            placed.append(placed_j)

        listed_words = held([P, I], U16, "listed_words")
        nc.vector.tensor_copy(listed_words[:], key_words[:].indirect(offsets[:]))
        listed_scales = held([P, I], U8, "listed_scales")
        nc.vector.tensor_copy(listed_scales[:], key_scales[:].indirect(offsets[:]))

        def quantise(grouped, name):
            width = grouped.shape[1]
            codes = held([P, width], U32, name + "_codes")
            scales = held([P, width], U8, name + "_scales")
            nc.vector.quantize_mx(codes[:].bitcast(FP8X4), scales[:], grouped.rearrange("p c r -> p (c r)"))
            return codes, scales

        query_by_place = query_raw[:].rearrange("p j (s r) -> p s j r", r=PACK)
        query_mx = []
        for pair in range(2):
            grouped = held([P, 2 * P, PACK], BF16, "query_grouped%d" % pair)
            src = query_by_place[:, :, :, 2 * pair : 2 * pair + 2]
            dst = grouped[:].rearrange("p (r s) j -> p s j r", r=2)
            if pair == 0:
                nc.vector.tensor_copy(dst, src)
            else:
                nc.scalar.copy(dst, src)
            query_mx.append(quantise(grouped[:], "query%d" % pair))

        placed_last = held([P, T], F32, "placed3", "query_grouped1")
        nc.gpsimd.memset(placed_last[:], 0.0)
        placed.append(placed_last)

        def group_heads(engine_copy, raw, name, tag=None):
            grouped = held([P, HALF_E, PACK], BF16, name, tag)
            for jj in range(2):
                cols = slice(jj * P, (jj + 1) * P)
                engine_copy(
                    grouped[:, cols, :].rearrange("p (c i) r -> p c r i", i=4),
                    raw[:, :, cols].rearrange("p r (c i) -> p c r i", i=4),
                )
            return grouped

        neg_max = held([P, PACK], F32, "neg_max")
        erase_grouped0 = group_heads(nc.scalar.copy, erase_raw[:, :, 0:HALF_E], "erase_grouped0")
        sums = erase_raw[:, 0, P : P + PACK]
        probs = held([P, PACK, I], F32, "probs")
        for r in range(PACK):
            scores = banks[r]
            codes, scales = query_mx[r // 2]
            cols = slice((r % 2) * P, (r % 2 + 1) * P)
            nc.tensor.matmul_mx(
                out=scores[:],
                lhsT=codes[:, cols].bitcast(FP8X4),
                lhsT_scale=scales[:, cols],
                rhs=listed_words[:].bitcast(FP4X4),
                rhs_scale=listed_scales[:],
                start=True,
                stop=True,
            )
            nc.vector.tensor_reduce(neg_max[:, r : r + 1], scores[:], AX.X, ALU.max, negate=True)
            nc.scalar.activation(
                probs[:, r, :], scores[:], ACT.Exp, bias=neg_max[:, r : r + 1], accum_out=sums[:, r : r + 1]
            )
        add_grouped0 = group_heads(nc.vector.tensor_copy, add_raw[:, :, 0:HALF_E], "add_grouped0", "query1_codes")
        heads_mx = [(quantise(erase_grouped0[:], "erase0"), quantise(add_grouped0[:], "add0"))]
        inv_sums = add_raw[:, 0, P : P + PACK]
        nc.vector.reciprocal(inv_sums, sums)
        gains = held([P, PACK], F32, "gains")
        nc.vector.tensor_tensor(gains[:], inv_sums, fac_cols[:], ALU.mult)

        w_codes = held([P, I], U32, "w_codes")
        w_scales = held([P, I], U8, "w_scales")
        gains_spread = gains[:].unsqueeze(1).unsqueeze(3).to_broadcast([P, HALF_I // 4, PACK, 4])
        w_rows = held([P, PACK, HALF_I], BF16, "w_rows")
        for r in range(PACK):
            nc.scalar.activation(w_rows[:, r, :], probs[:, r, HALF_I:I], ACT.Copy, scale=gains[:, r : r + 1])
        for half in range(2):
            cols = slice(half * HALF_I, (half + 1) * HALF_I)
            w_grouped = held([P, HALF_I, PACK], BF16, "w_grouped%d" % half)
            if half == 0:
                nc.vector.tensor_tensor(
                    w_grouped[:].rearrange("p (c i) r -> p c r i", i=4),
                    probs[:, :, cols].rearrange("p r (c i) -> p c r i", i=4),
                    gains_spread,
                    ALU.mult,
                )
            else:
                nc.vector.tensor_copy(
                    w_grouped[:].rearrange("p (c i) r -> p c r i", i=4),
                    w_rows[:].rearrange("p r (c i) -> p c r i", i=4),
                )
            nc.vector.quantize_mx(
                w_codes[:, cols].bitcast(FP8X4), w_scales[:, cols], w_grouped[:].rearrange("p i r -> p (i r)")
            )

        nc.tensor.transpose(banks[3][:, 0:P], vec_rows[:], identity[:])
        retain_cols = held([P, T_BLOCKS], F32, "retain_cols")
        nc.scalar.copy(retain_cols[:], banks[3][:, 0:T_BLOCKS])
        neg_ef_cols = held([P, E_TILES], F32, "neg_ef_cols")
        nc.scalar.activation(neg_ef_cols[:], banks[3][:, T_BLOCKS : T_BLOCKS + E_TILES], ACT.Copy, scale=-1.0)

        def retain_turned(turn_banks):
            turned = held([P, T_BLOCKS, E], F32, "retained_t")
            for b in range(T_BLOCKS):
                bank = turn_banks[b % len(turn_banks)]
                for j in range(E_TILES):
                    nc.tensor.transpose(bank[:, j * P : (j + 1) * P], mem_tiles[j][:, b * P : (b + 1) * P], identity[:])
                nc.scalar.activation(turned[:, b, :], bank[:], ACT.Copy, scale=retain_cols[:, b : b + 1])
            return turned

        def head_sum(which, j, cols, bank):
            codes, scales = heads_mx[j // 2][which]
            e_cols = slice((j % 2) * P, (j % 2 + 1) * P)
            total = bank[:, 0 : cols.stop - cols.start]
            nc.tensor.matmul_mx(
                out=total,
                lhsT=codes[:, e_cols].bitcast(FP8X4),
                lhsT_scale=scales[:, e_cols],
                rhs=w_codes[:, cols].bitcast(FP8X4),
                rhs_scale=w_scales[:, cols],
                start=True,
                stop=True,
            )
            return total

        def listed(cols):
            return offsets[:, cols.start // 16 : cols.stop // 16]

        def erase_listed(j, cols, bank, left_tag=None):
            width = cols.stop - cols.start
            kept = held([P, width], F32, "kept%d_%d" % (j, cols.start))
            nc.scalar.activation(
                kept[:], head_sum(0, j, cols, bank), ACT.Identity, bias=one_col[:], scale=neg_ef_cols[:, j : j + 1]
            )
            left = held([P, width], F32, "left%d_%d" % (j, cols.start), left_tag)
            nc.vector.tensor_tensor(left[:], mem_tiles[j][:].indirect(listed(cols)), kept[:], ALU.mult)
            return left

        def add_and_place(j, cols, bank, left):
            added = held([P, cols.stop - cols.start], F32, "added%d_%d" % (j, cols.start))
            nc.scalar.copy(added[:], head_sum(1, j, cols, bank))
            nc.vector.tensor_tensor(placed[j][:].indirect(listed(cols)), left[:], added[:], ALU.add)

        def turn_back(rows_t, bank, start, stop):
            for n in range(4):
                nc.tensor.matmul(
                    bank[:, n * P : (n + 1) * P],
                    rows_t[n],
                    identity[:],
                    start=start and n == 0,
                    stop=stop and n == 3,
                    is_transpose=True,
                )

        def retained_blocks(j, half):
            return [retained_t[:, 4 * half + n, j * P : (j + 1) * P] for n in range(4)]

        def store(queue, j, half, result):
            queue.dma_start(out[j * P : (j + 1) * P, half * BANK : (half + 1) * BANK], result[:])

        def finish_on_vector(j, half, back_bank):
            result = held([P, BANK], F32, "result%d_%d" % (j, half))
            nc.vector.tensor_tensor(result[:], back_bank[:], placed[j][:, half * BANK : (half + 1) * BANK], ALU.add)
            store(nc.sync, j, half, result)

        def finish_on_tensor(j, halves, back_banks, turn_banks):
            placed_t = []
            for half, back_bank, turn_bank in zip(halves, back_banks, turn_banks):
                turn_back(retained_blocks(j, half), back_bank, True, False)
                for n in range(4):
                    b = 4 * half + n
                    nc.tensor.transpose(turn_bank[:, n * P : (n + 1) * P], placed[j][:, b * P : (b + 1) * P], identity[:])
                turned = held([P, BANK], F32, "placed_t%d_%d" % (j, half))
                nc.scalar.copy(turned[:], turn_bank[:])
                placed_t.append(turned)
            for half, back_bank, turned in zip(halves, back_banks, placed_t):
                turn_back([turned[:, n * P : (n + 1) * P] for n in range(4)], back_bank, False, True)
                result = held([P, BANK], F32, "result%d_%d" % (j, half))
                nc.scalar.copy(result[:], back_bank[:])
                store(nc.scalar, j, half, result)

        first, second, whole = slice(0, HALF_I), slice(HALF_I, I), slice(0, I)
        add_and_place(0, first, banks[5], erase_listed(0, first, banks[4]))
        erase_grouped1 = group_heads(nc.scalar.copy, erase_raw[:, :, HALF_E:E], "erase_grouped1", "neg_max")
        add_grouped1 = group_heads(nc.scalar.copy, add_raw[:, :, HALF_E:E], "add_grouped1", "fac_cols")
        heads_mx.append((quantise(erase_grouped1[:], "erase1"), quantise(add_grouped1[:], "add1")))
        left0 = erase_listed(0, second, banks[6], "fac_cols")
        left1 = erase_listed(1, whole, banks[2])
        add_and_place(0, second, banks[7], left0)
        left2 = erase_listed(2, whole, banks[4])
        add_and_place(1, whole, banks[3], left1)
        retained_t = retain_turned(banks[0:2])
        left3 = erase_listed(3, whole, banks[6])
        add_and_place(2, whole, banks[5], left2)
        add_and_place(3, whole, banks[7], left3)
        on_vector = [(2, 1, banks[5]), (3, 0, banks[6]), (3, 1, banks[7])]
        finish_on_tensor(0, (0, 1), banks[2:4], banks[0:2])
        finish_on_tensor(1, (0, 1), banks[2:4], banks[0:2])
        for j, half, bank in on_vector:
            turn_back(retained_blocks(j, half), bank, True, True)
        finish_on_tensor(2, (0,), banks[4:5], banks[3:4])
        for j, half, bank in on_vector:
            finish_on_vector(j, half, bank)
